import numpy as np
import ml_dtypes


def mxq(x, axis, fmt="e4m3"):
    dtype, down = {"e4m3": (ml_dtypes.float8_e4m3fn, 7), "e5m2": (ml_dtypes.float8_e5m2, 14)}[fmt]
    v = np.moveaxis(np.asarray(x, np.float32).astype(ml_dtypes.bfloat16).astype(np.float64), axis, -1)
    blocks = v.reshape(v.shape[:-1] + (-1, 32))
    amax = np.abs(blocks).max(-1, keepdims=True)
    byte = np.maximum(np.where(amax > 0, np.frexp(amax)[1] - 1 + 127, 0) - down, 1)
    scale = np.exp2(byte - 127.0)
    codes = (blocks / scale).astype(np.float32).astype(dtype).astype(np.float64)
    return np.moveaxis((codes * scale).reshape(v.shape), -1, axis)


WIDE = False


def mx_kscale(k):
    if not WIDE:
        return np.ones(k)
    levels = np.array([10, -10, 5, -5, 0])
    if k % 512:
        return np.exp2(np.random.permutation(np.resize(levels, k // 32))).repeat(32)
    a = np.empty((k // 512, 16))
    for p in range(k // 512):
        a[p, :8] = np.random.permutation(np.resize(levels, 8))
        for g in range(8):
            far = levels[np.abs(levels - a[p, g]) >= 10]
            a[p, g + 8] = far[np.random.randint(len(far))]
    return np.exp2(a.ravel()).repeat(32)


def f64(x):
    return np.asarray(x).astype(np.float64)


def striped(idx):
    return np.tile(np.asarray(idx).reshape(-1, 16).T, (8, 1)).astype(np.uint16)


def unstriped(offs):
    return offs[:16].T.reshape(-1).astype(np.int64)


E2M1 = np.array([0.0, 0.5, 1.0, 1.5, 2.0, 3.0, 4.0, 6.0, -0.0, -0.5, -1.0, -1.5, -2.0, -3.0, -4.0, -6.0])


def pack_weight(w, fmt):
    k, n = w.shape
    w = f64(np.asarray(w, np.float32).astype(ml_dtypes.bfloat16)).reshape(k // 32, 32, n)
    amax = np.abs(w).max(1)
    if fmt == "e4m3":
        byte = np.frexp(amax)[1] - 1 + 127 - 7
    else:
        mant, ex = np.frexp(amax / 6.0)
        byte = np.where(mant > 0.5, ex, ex - 1) + 127
    byte = np.clip(np.where(amax > 0, byte, 1), 1, 254)
    scaled = (w * np.exp2(127.0 - byte)[:, None, :]).reshape(k, n).astype(np.float32)
    by_word = np.ascontiguousarray(scaled.reshape(k // 512, 128, 4, n).transpose(0, 1, 3, 2))
    if fmt == "e4m3":
        words = by_word.astype(ml_dtypes.float8_e4m3fn).view(np.uint8)
    else:
        c = by_word.astype(ml_dtypes.float4_e2m1fn).view(np.uint8) & 0xF
        words = (c[..., 0::2] | (c[..., 1::2] << 4)).reshape(k // 512, 128, 2 * n)
    return np.ascontiguousarray(words), np.ascontiguousarray(byte.astype(np.uint8).reshape(k // 512, 16, n))


def unpack_weight(words, scales, fmt):
    g, _, n = scales.shape
    words = np.ascontiguousarray(words).reshape(g, 128, n, -1)
    if fmt == "e4m3":
        vals = words.view(ml_dtypes.float8_e4m3fn).astype(np.float64)
    else:
        nib = np.empty((g, 128, n, 4), np.uint8)
        nib[..., 0::2] = words & 0xF
        nib[..., 1::2] = words >> 4
        vals = E2M1[nib]
    vals = vals * np.repeat(np.exp2(scales.astype(np.float64) - 127.0), 8, axis=1)[..., None]
    return vals.transpose(0, 1, 3, 2).reshape(g * 512, n)


def bf(x):
    return np.asarray(x, np.float32).astype(ml_dtypes.bfloat16)


def planes(Y):
    r, m = Y.shape
    b = f64(bf(Y)).reshape(r // 32, 32, m)
    amax = np.abs(b).max(1)
    byte = np.clip(np.where(amax > 0, np.frexp(amax)[1] - 1 + 127 - 7, 1), 1, 254)
    codes = (b * np.exp2(127.0 - byte)[:, None, :]).reshape(r, m).astype(np.float32).astype(ml_dtypes.float8_e4m3fn).view(np.uint8)
    words = codes.reshape(r // 512, 128, 4, m).transpose(0, 1, 3, 2)
    return np.ascontiguousarray(words), np.ascontiguousarray(byte.astype(np.uint8).reshape(r // 512, 16, m))


D, T, I, J, U, Z, E, M, C = 512, 2048, 512, 256, 1024, 1024, 512, 1024, 512


def setup_inputs():
    n = np.random.standard_normal
    idx = np.random.permutation(T)[:I]
    idx2 = np.random.permutation(U)[:J]
    idx3 = np.random.permutation(Z)[:J]
    idx4 = np.random.permutation(M)[:J]
    fd = mx_kscale(D)
    fi = mx_kscale(I)
    fc = mx_kscale(C)
    ti = np.ones(T)
    ti[idx] = fi
    keysp = pack_weight(n((D, T)) / fd[:, None], "e2m1")
    return {
        "keys_words": keysp[0],
        "keys_scales": keysp[1],
        "notes": (n((D, U)) * 1.0 / np.sqrt(D) * fd[:, None]).astype(np.float32),
        "users2": (n((D, Z)) * 1.0 / np.sqrt(D) * fd[:, None]).astype(np.float32),
        "rowf": (np.random.uniform(0.02, 0.08, (I, 1)) * fi[:, None]).astype(np.float32),
        "vals": (n((E, T)) / ti).astype(np.float32),
        "wm": (n((C, E)) * 1.0 / np.sqrt(C) * fc[:, None]).astype(np.float32),
        "mstore": (n((C, M)) / fc[:, None]).astype(np.float32),
        "offs": striped(idx),
        "offs2": striped(idx2),
        "offs3": striped(idx3),
        "offs4": striped(idx4),
    }


def reference(keys_words, keys_scales, notes, users2, rowf, vals, wm, mstore, offs, offs2, offs3, offs4):
    idx = unstriped(offs)
    idx2 = unstriped(offs2)
    idx3 = unstriped(offs3)
    idx4 = unstriped(offs4)
    keysu = unpack_weight(keys_words, keys_scales, "e2m1")
    keysidxg = keysu[:, idx]
    notesidx2q = mxq(f64(notes)[:, idx2], 0, "e4m3")
    g1 = keysidxg.T @ notesidx2q
    users2idx3q = mxq(f64(users2)[:, idx3], 0, "e4m3")
    g2 = keysidxg.T @ users2idx3q
    g0 = np.maximum(g1, g2)
    gr1 = g0 * f64(rowf)
    vt1 = f64(vals)[:, idx].T
    vt1q = mxq(vt1, 0, "e4m3")
    gr1q = mxq(gr1, 0, "e4m3")
    o = vt1q.T @ gr1q
    wmq = mxq(f64(wm), 0, "e4m3")
    mstoreq = mxq(f64(mstore), 0, "e4m3")
    me = wmq.T @ mstoreq
    y = o * me[:, idx4]
    words, scales = planes(y)
    return y, words, scales

@@ -1,0 +1,256 @@
+from contextlib import ExitStack
+
+import concourse.mybir as mybir
+from concourse.masks import make_identity
+
+D, T, I, J, U, Z, E, M, C = 512, 2048, 512, 256, 1024, 1024, 512, 1024, 512
+FLOPS = 2 * (2 * D * I * J + I * E * J + C * E * M)
+
+F32 = mybir.dt.float32
+BF16 = mybir.dt.bfloat16
+I32 = mybir.dt.int32
+U32 = mybir.dt.uint32
+U16 = mybir.dt.uint16
+U8 = mybir.dt.uint8
+FP8X4 = mybir.dt.float8_e4m3fn_x4
+FP4X4 = mybir.dt.float4_e2m1fn_x4
+COPY = mybir.ActivationFunctionType.Copy
+MULT = mybir.AluOpType.mult
+MAX = mybir.AluOpType.max
+
+P = 128
+PACK = 4
+BANK = 512
+ALIGN = 64
+KB = 1024
+PLACES = {
+    "ms_grouped1": 0,
+    "picked_words": 0,
+    "dealt_scales": KB,
+    "ms_codes1": 4 * KB,
+    "notes_picked": 4 * KB,
+    "notes_codes": 8 * KB,
+    "memory3": 9 * KB,
+    "users_picked": 8 * KB,
+    "vals_picked0": 8 * KB,
+    "vals_picked1": 8 * KB,
+    "vals_picked2": 8 * KB,
+    "picked_memory1": 13 * KB,
+    "vals_picked3": 13 * KB,
+    "gr_grouped": 14 * KB,
+    "vt_codes0": 14 * KB,
+    "vt_codes1": 14 * KB + KB // 2,
+    "vt_codes2": 15 * KB,
+    "vt_codes3": 15 * KB + KB // 2,
+}
+
+
+def tile_attend_tab_larger_gains_pl_kernel(
+    tc, keys_words, keys_scales, notes, users2, rowf, vals, wm, mstore, offs, offs2, offs3, offs4, out_0, out_1, out_2
+):
+    nc = tc.nc
+    with ExitStack() as ctx:
+        keep = ctx.enter_context(tc.tile_pool(name="keep", bufs=1))
+        reused = ctx.enter_context(tc.tile_pool(name="reused", bufs=1))
+        psum = ctx.enter_context(tc.psum_pool(name="psum", bufs=1))
+
+        def held(name, shape, dtype):
+            if name in PLACES:
+                return reused.tile(shape, dtype, name=name, align_bytes=ALIGN, offset=PLACES[name])
+            return keep.tile(shape, dtype, name=name, align_bytes=ALIGN)
+
+        def gather(engine, out, window, offsets):
+            if engine == "vector":
+                nc.vector.tensor_copy(out, window.indirect(offsets))
+            else:
+                nc.scalar.activation(out, window.indirect(offsets), COPY)
+
+        def quantize(codes, scales, grouped):
+            nc.vector.quantize_mx(out=codes.bitcast(FP8X4), scales=scales, in_=grouped)
+
+        wm_raw = held("wm_raw", [P, PACK * E], F32)
+        ms_raw = [held(f"ms_raw{h}", [P, PACK * BANK], F32) for h in range(M // BANK)]
+        list_i = held("list_i", [P, I // 16], U16)
+        list_n = held("list_n", [P, J // 16], U16)
+        list_u = held("list_u", [P, J // 16], U16)
+        list_m = held("list_m", [P, J // 16], U16)
+        row_factor = held("row_factor", [P, PACK], F32)
+        key_words = held("key_words", [P, T], U16)
+        key_scales = held("key_scales", [P, T], U8)
+        notes_raw = [held(f"notes_raw{u}", [P, 2 * U], F32) for u in range(2)]
+        users_raw = [held(f"users_raw{u}", [P, 2 * Z], F32) for u in range(2)]
+        vals_raw = [held(f"vals_raw{t}", [P, T], F32) for t in range(PACK)]
+        identity = held("identity", [P, P], F32)
+
+        nc.vector.memset(key_scales[:].bitcast(I32), 0)
+        nc.gpsimd.dma_start(row_factor[:], rowf.rearrange("(p t) o -> p (t o)", t=PACK))
+        make_identity(nc, identity[:])
+
+        nc.sync.dma_start(wm_raw[:], wm.rearrange("(p t) e -> p (t e)", t=PACK))
+        ms_planes = mstore.rearrange("(p t) m -> p t m", t=PACK)
+        for h in range(M // BANK):
+            nc.sync.dma_start(
+                ms_raw[h][:].rearrange("p (t m) -> p t m", t=PACK), ms_planes[:, :, h * BANK : (h + 1) * BANK]
+            )
+        nc.sync.dma_start(list_m[:], offs4)
+        nc.sync.dma_start(list_i[:], offs)
+        nc.sync.dma_start(key_words[:].bitcast(I32), keys_words[0].bitcast(I32))
+        nc.sync.dma_start(list_n[:], offs2)
+        nc.sync.dma_start(list_u[:], offs3)
+        for q in range(4):
+            nc.sync.dma_start(
+                key_scales[32 * q : 32 * q + 4, :].bitcast(I32), keys_scales[0, 4 * q : 4 * q + 4, :].bitcast(I32)
+            )
+        for raw, source in ((notes_raw, notes), (users_raw, users2)):
+            pairs = source.rearrange("(p u e) n -> u p (e n)", u=2, e=2)
+            for u in range(2):
+                nc.sync.dma_start(raw[u][:], pairs[u])
+        vals_planes = vals.rearrange("(p t) n -> t p n", t=PACK)
+        for t in range(PACK):
+            nc.sync.dma_start(vals_raw[t][:], vals_planes[t])
+
+        wm_grouped = held("wm_grouped", [P, PACK * E], BF16)
+        wm_codes = held("wm_codes", [P, E], U32)
+        wm_scales = held("wm_scales", [P, E], U8)
+        nc.vector.tensor_copy(
+            wm_grouped[:].rearrange("p (r m t) -> p m r t", r=PACK, t=PACK),
+            wm_raw[:].rearrange("p (t m r) -> p m r t", t=PACK, r=PACK),
+        )
+        quantize(wm_codes[:], wm_scales[:], wm_grouped[:])
+
+        memory = [held(f"memory{r}", [P, M], F32) for r in range(PACK)]
+        for h in range(M // BANK):
+            cols = slice(h * BANK, (h + 1) * BANK)
+            ms_grouped = held(f"ms_grouped{h}", [P, PACK * BANK], BF16)
+            ms_codes = held(f"ms_codes{h}", [P, BANK], U32)
+            ms_scales = held(f"ms_scales{h}", [P, BANK], U8)
+            nc.vector.tensor_copy(
+                ms_grouped[:].rearrange("p (m t) -> p m t", t=PACK), ms_raw[h][:].rearrange("p (t m) -> p m t", t=PACK)
+            )
+            quantize(ms_codes[:], ms_scales[:], ms_grouped[:])
+            for r in range(PACK):
+                rows = slice(r * P, (r + 1) * P)
+                bank = psum.tile([P, BANK], F32, name="bank", tag="wide", bufs=4)
+                nc.tensor.matmul_mx(
+                    out=bank[:],
+                    lhsT=wm_codes[:, rows].bitcast(FP8X4),
+                    lhsT_scale=wm_scales[:, rows],
+                    rhs=ms_codes[:].bitcast(FP8X4),
+                    rhs_scale=ms_scales[:],
+                    start=True,
+                    stop=True,
+                )
+                nc.scalar.copy(memory[r][:, cols], bank[:])
+
+        picked_words = held("picked_words", [P, I], U16)
+        dealt_words = held("dealt_words", [P, I], U16)
+        dealt_scales = held("dealt_scales", [P, I], U8)
+        gather("vector", picked_words[:], key_words[:], list_i[:])
+        gather("vector", dealt_scales[:].rearrange("p (r s) -> p s r", r=PACK), key_scales[:], list_i[:])
+        nc.vector.tensor_copy(
+            dealt_words[:].rearrange("p (r s) -> p r s", r=PACK), picked_words[:].rearrange("p (s r) -> p r s", r=PACK)
+        )
+
+        def scores(name, raw, width, offsets, on_scalar):
+            picked = held(name + "_picked", [P, PACK * J], F32)
+            grouped = held(name + "_grouped", [P, PACK * J], BF16)
+            codes = held(name + "_codes", [P, J], U32)
+            scales = held(name + "_scales", [P, J], U8)
+            for t in range(PACK):
+                engine = "scalar" if t in on_scalar else "vector"
+                gather(engine, picked[:, t * J : (t + 1) * J], raw[t // 2][:, t % 2 * width : (t % 2 + 1) * width], offsets)
+            nc.vector.tensor_copy(
+                grouped[:].rearrange("p (j t) -> p j t", t=PACK), picked[:].rearrange("p (t j) -> p j t", t=PACK)
+            )
+            quantize(codes[:], scales[:], grouped[:])
+            banks = []
+            for pair in range(PACK // 2):
+                bank = psum.tile([P, BANK], F32, name="bank", tag="wide", bufs=4)
+                for half in range(2):
+                    r = 2 * pair + half
+                    slots = slice(r * P, (r + 1) * P)
+                    nc.tensor.matmul_mx(
+                        out=bank[:, half * J : (half + 1) * J],
+                        lhsT=dealt_words[:, slots].bitcast(FP4X4),
+                        lhsT_scale=dealt_scales[:, slots],
+                        rhs=codes[:].bitcast(FP8X4),
+                        rhs_scale=scales[:],
+                        start=True,
+                        stop=True,
+                    )
+                banks.append(bank)
+            return banks
+
+        g1 = held("g1", [P, PACK * J], F32)
+        for pair, bank in enumerate(scores("notes", notes_raw, U, list_n[:], (1, 3))):
+            nc.scalar.copy(g1[:, pair * BANK : (pair + 1) * BANK], bank[:])
+
+        picked_memory = [held(f"picked_memory{r}", [P, J], F32) for r in range(PACK)]
+        for r in range(PACK):
+            gather("scalar", picked_memory[r][:], memory[r][:], list_m[:])
+
+        g0 = held("g0", [P, PACK * J], F32)
+        gr_rows = held("gr_rows", [P, PACK * J], BF16)
+        gr_grouped = held("gr_grouped", [P, PACK * J], BF16)
+        gr_codes = held("gr_codes", [P, J], U32)
+        gr_scales = held("gr_scales", [P, J], U8)
+        for pair, bank in enumerate(scores("users", users_raw, Z, list_u[:], (3,))):
+            cols = slice(pair * BANK, (pair + 1) * BANK)
+            nc.vector.tensor_tensor(g0[:, cols], bank[:], g1[:, cols], MAX)
+        for r in range(PACK):
+            cols = slice(r * J, (r + 1) * J)
+            nc.vector.tensor_scalar(gr_rows[:, cols], g0[:, cols], row_factor[:, r : r + 1], None, MULT)
+        nc.vector.tensor_copy(
+            gr_grouped[:].rearrange("p (j t) -> p j t", t=PACK), gr_rows[:].rearrange("p (t j) -> p j t", t=PACK)
+        )
+        quantize(gr_codes[:], gr_scales[:], gr_grouped[:])
+
+        y = held("y", [P, PACK * J], F32)
+        y_grouped = held("y_grouped", [P, PACK * J], BF16)
+        y_codes = held("y_codes", [P, J], U32)
+        y_scales = held("y_scales", [P, J], U8)
+        y_rows = out_0.rearrange("(p r) j -> p (r j)", r=PACK)
+        for r in range(PACK):
+            picked = held(f"vals_picked{r}", [P, I], BF16)
+            if r < PACK - 1:
+                gather("scalar", picked[:], vals_raw[r][:], list_i[:])
+            else:
+                gather("vector", picked[:, : I // 2], vals_raw[r][:], list_i[:, : I // 32])
+                gather("scalar", picked[:, I // 2 :], vals_raw[r][:], list_i[:, I // 32 :])
+            turned = psum.tile([P, 2 * P], F32, name="turned", tag="turned", bufs=2)
+            words = picked[:].bitcast(F32)
+            for u in range(2):
+                nc.tensor.transpose(turned[:, u * P : (u + 1) * P], words[:, u::2], identity[:])
+            vt_grouped = held(f"vt_grouped{r}", [P, PACK * P], BF16)
+            vt_codes = held(f"vt_codes{r}", [P, P], U32)
+            vt_scales = held(f"vt_scales{r}", [P, P], U8)
+            nc.scalar.copy(
+                vt_grouped[:].bitcast(F32).rearrange("p (m u) -> p m u", u=2),
+                turned[:].rearrange("p (u m) -> p m u", u=2),
+            )
+            quantize(vt_codes[:], vt_scales[:], vt_grouped[:])
+            product = psum.tile([P, J], F32, name="product", tag="product", bufs=2)
+            nc.tensor.matmul_mx(
+                out=product[:],
+                lhsT=vt_codes[:].bitcast(FP8X4),
+                lhsT_scale=vt_scales[:],
+                rhs=gr_codes[:].bitcast(FP8X4),
+                rhs_scale=gr_scales[:],
+                start=True,
+                stop=True,
+            )
+            cols = slice(r * J, (r + 1) * J)
+            nc.vector.tensor_tensor(y[:, cols], product[:], picked_memory[r][:], MULT)
+            nc.sync.dma_start(y_rows[:, cols], y[:, cols])
+            if r % 2 == 1:
+                nc.vector.tensor_copy(
+                    y_grouped[:].rearrange("p (j t) -> p j t", t=PACK)[:, :, r - 1 : r + 1],
+                    y[:].rearrange("p (t j) -> p j t", t=PACK)[:, :, r - 1 : r + 1],
+                )
+        quantize(y_codes[:], y_scales[:], y_grouped[:])
+        nc.sync.dma_start(out_1[0].rearrange("p c r -> p (c r)").bitcast(I32), y_codes[:].bitcast(I32))
+        for q in range(4):
+            queue = nc.sync if q % 2 == 0 else nc.scalar
+            queue.dma_start(
+                out_2[0, 4 * q : 4 * q + 4, :].bitcast(I32), y_scales[32 * q : 32 * q + 4, :].bitcast(I32)
+            )

@@ -29,19 +29,23 @@ PLACES = {
     "dealt_scales": KB,
     "ms_codes1": 4 * KB,
     "notes_picked": 4 * KB,
-    "notes_codes": 8 * KB,
-    "memory3": 9 * KB,
+    "notes_grouped": 8 * KB,
     "users_picked": 8 * KB,
     "vals_picked0": 8 * KB,
-    "vals_picked1": 8 * KB,
-    "vals_picked2": 8 * KB,
-    "picked_memory1": 13 * KB,
-    "vals_picked3": 13 * KB,
+    "vals_picked1": 9 * KB,
+    "vt_grouped0": 12 * KB,
+    "vals_picked2": 12 * KB,
     "gr_grouped": 14 * KB,
     "vt_codes0": 14 * KB,
     "vt_codes1": 14 * KB + KB // 2,
-    "vt_codes2": 15 * KB,
-    "vt_codes3": 15 * KB + KB // 2,
+    "notes_raw1": 16 * KB,
+    "picked_memory0": 16 * KB,
+    "picked_memory2": 17 * KB,
+    "picked_memory3": 18 * KB,
+    "picked_memory1": 19 * KB,
+    "vals_picked3": 19 * KB,
+    "vals_raw3": 24 * KB,
+    "vt_grouped2": 24 * KB,
 }
 
 
@@ -53,6 +57,7 @@ def tile_attend_tab_larger_gains_pl_kernel(
         keep = ctx.enter_context(tc.tile_pool(name="keep", bufs=1))
         reused = ctx.enter_context(tc.tile_pool(name="reused", bufs=1))
         psum = ctx.enter_context(tc.psum_pool(name="psum", bufs=1))
+        ring = ctx.enter_context(tc.psum_pool(name="ring", bufs=1))
 
         def held(name, shape, dtype):
             if name in PLACES:
@@ -217,7 +222,7 @@ def tile_attend_tab_larger_gains_pl_kernel(
             else:
                 gather("vector", picked[:, : I // 2], vals_raw[r][:], list_i[:, : I // 32])
                 gather("scalar", picked[:, I // 2 :], vals_raw[r][:], list_i[:, I // 32 :])
-            turned = psum.tile([P, 2 * P], F32, name="turned", tag="turned", bufs=2)
+            turned = ring.tile([P, 2 * P], F32, name=f"turned{r}", offset=2 * r % 3 * 2 * KB)
             words = picked[:].bitcast(F32)
             for u in range(2):
                 nc.tensor.transpose(turned[:, u * P : (u + 1) * P], words[:, u::2], identity[:])
@@ -229,7 +234,7 @@ def tile_attend_tab_larger_gains_pl_kernel(
                 turned[:].rearrange("p (u m) -> p m u", u=2),
             )
             quantize(vt_codes[:], vt_scales[:], vt_grouped[:])
-            product = psum.tile([P, J], F32, name="product", tag="product", bufs=2)
+            product = ring.tile([P, J], F32, name=f"product{r}", offset=(2 * r + 1) % 3 * 2 * KB)
             nc.tensor.matmul_mx(
                 out=product[:],
                 lhsT=vt_codes[:].bitcast(FP8X4),

@@ -33,8 +33,9 @@ PLACES = {
     "users_picked": 8 * KB,
     "vals_picked0": 8 * KB,
     "vals_picked1": 9 * KB,
-    "vt_grouped0": 12 * KB,
-    "vals_picked2": 12 * KB,
+    "vals_raw1": 32 * KB,
+    "vt_grouped0": 32 * KB,
+    "vals_picked2": 32 * KB,
     "gr_grouped": 14 * KB,
     "vt_codes0": 14 * KB,
     "vt_codes1": 14 * KB + KB // 2,
@@ -46,6 +47,7 @@ PLACES = {
     "vals_picked3": 19 * KB,
     "vals_raw3": 24 * KB,
     "vt_grouped2": 24 * KB,
+    "y_grouped": 26 * KB,
 }
 
 
@@ -73,6 +75,12 @@ def tile_attend_tab_larger_gains_pl_kernel(
         def quantize(codes, scales, grouped):
             nc.vector.quantize_mx(out=codes.bitcast(FP8X4), scales=scales, in_=grouped)
 
+        def group_pair(grouped, planes, u, cols=slice(0, J)):
+            nc.vector.tensor_copy(
+                grouped[:].rearrange("p (j t) -> p j t", t=PACK)[:, cols, 2 * u : 2 * u + 2],
+                planes[:].rearrange("p (t j) -> p j t", t=PACK)[:, cols, 2 * u : 2 * u + 2],
+            )
+
         wm_raw = held("wm_raw", [P, PACK * E], F32)
         ms_raw = [held(f"ms_raw{h}", [P, PACK * BANK], F32) for h in range(M // BANK)]
         list_i = held("list_i", [P, I // 16], U16)
@@ -91,17 +99,15 @@ def tile_attend_tab_larger_gains_pl_kernel(
         nc.gpsimd.dma_start(row_factor[:], rowf.rearrange("(p t) o -> p (t o)", t=PACK))
         make_identity(nc, identity[:])
 
+        ms_planes = mstore.rearrange("(p t) (h m) -> h p t m", t=PACK, m=BANK)
         nc.sync.dma_start(wm_raw[:], wm.rearrange("(p t) e -> p (t e)", t=PACK))
-        ms_planes = mstore.rearrange("(p t) m -> p t m", t=PACK)
-        for h in range(M // BANK):
-            nc.sync.dma_start(
-                ms_raw[h][:].rearrange("p (t m) -> p t m", t=PACK), ms_planes[:, :, h * BANK : (h + 1) * BANK]
-            )
+        nc.sync.dma_start(ms_raw[0][:].rearrange("p (t m) -> p t m", t=PACK), ms_planes[0])
         nc.sync.dma_start(list_m[:], offs4)
         nc.sync.dma_start(list_i[:], offs)
-        nc.sync.dma_start(key_words[:].bitcast(I32), keys_words[0].bitcast(I32))
         nc.sync.dma_start(list_n[:], offs2)
         nc.sync.dma_start(list_u[:], offs3)
+        nc.sync.dma_start(ms_raw[1][:].rearrange("p (t m) -> p t m", t=PACK), ms_planes[1])
+        nc.sync.dma_start(key_words[:].bitcast(I32), keys_words[0].bitcast(I32))
         for q in range(4):
             nc.sync.dma_start(
                 key_scales[32 * q : 32 * q + 4, :].bitcast(I32), keys_scales[0, 4 * q : 4 * q + 4, :].bitcast(I32)
@@ -129,9 +135,13 @@ def tile_attend_tab_larger_gains_pl_kernel(
             ms_grouped = held(f"ms_grouped{h}", [P, PACK * BANK], BF16)
             ms_codes = held(f"ms_codes{h}", [P, BANK], U32)
             ms_scales = held(f"ms_scales{h}", [P, BANK], U8)
-            nc.vector.tensor_copy(
-                ms_grouped[:].rearrange("p (m t) -> p m t", t=PACK), ms_raw[h][:].rearrange("p (t m) -> p m t", t=PACK)
-            )
+            target = ms_grouped[:].rearrange("p (m t) -> p m t", t=PACK)
+            source = ms_raw[h][:].rearrange("p (t m) -> p m t", t=PACK)
+            if h == 0:
+                nc.vector.tensor_copy(target[:, : BANK // 2, :], source[:, : BANK // 2, :])
+                nc.scalar.copy(target[:, BANK // 2 :, :], source[:, BANK // 2 :, :])
+            else:
+                nc.vector.tensor_copy(target, source)
             quantize(ms_codes[:], ms_scales[:], ms_grouped[:])
             for r in range(PACK):
                 rows = slice(r * P, (r + 1) * P)
@@ -164,9 +174,8 @@ def tile_attend_tab_larger_gains_pl_kernel(
             for t in range(PACK):
                 engine = "scalar" if t in on_scalar else "vector"
                 gather(engine, picked[:, t * J : (t + 1) * J], raw[t // 2][:, t % 2 * width : (t % 2 + 1) * width], offsets)
-            nc.vector.tensor_copy(
-                grouped[:].rearrange("p (j t) -> p j t", t=PACK), picked[:].rearrange("p (t j) -> p j t", t=PACK)
-            )
+                if t % 2 == 1:
+                    group_pair(grouped, picked, t // 2)
             quantize(codes[:], scales[:], grouped[:])
             banks = []
             for pair in range(PACK // 2):
@@ -215,17 +224,23 @@ def tile_attend_tab_larger_gains_pl_kernel(
         y_codes = held("y_codes", [P, J], U32)
         y_scales = held("y_scales", [P, J], U8)
         y_rows = out_0.rearrange("(p r) j -> p (r j)", r=PACK)
-        for r in range(PACK):
+        turned_bank = (0, 1, 1, 0)
+        product_bank = (1, 0, 2, 1)
+
+        def turn(r):
             picked = held(f"vals_picked{r}", [P, I], BF16)
             if r < PACK - 1:
                 gather("scalar", picked[:], vals_raw[r][:], list_i[:])
             else:
                 gather("vector", picked[:, : I // 2], vals_raw[r][:], list_i[:, : I // 32])
                 gather("scalar", picked[:, I // 2 :], vals_raw[r][:], list_i[:, I // 32 :])
-            turned = ring.tile([P, 2 * P], F32, name=f"turned{r}", offset=2 * r % 3 * 2 * KB)
+            turned = ring.tile([P, 2 * P], F32, name=f"turned{r}", offset=turned_bank[r] * 2 * KB)
             words = picked[:].bitcast(F32)
             for u in range(2):
                 nc.tensor.transpose(turned[:, u * P : (u + 1) * P], words[:, u::2], identity[:])
+            return turned
+
+        def quantize_values(r, turned):
             vt_grouped = held(f"vt_grouped{r}", [P, PACK * P], BF16)
             vt_codes = held(f"vt_codes{r}", [P, P], U32)
             vt_scales = held(f"vt_scales{r}", [P, P], U8)
@@ -234,7 +249,10 @@ def tile_attend_tab_larger_gains_pl_kernel(
                 turned[:].rearrange("p (u m) -> p m u", u=2),
             )
             quantize(vt_codes[:], vt_scales[:], vt_grouped[:])
-            product = ring.tile([P, J], F32, name=f"product{r}", offset=(2 * r + 1) % 3 * 2 * KB)
+            return vt_codes, vt_scales
+
+        def multiply(r, vt_codes, vt_scales):
+            product = ring.tile([P, J], F32, name=f"product{r}", offset=product_bank[r] * 2 * KB)
             nc.tensor.matmul_mx(
                 out=product[:],
                 lhsT=vt_codes[:].bitcast(FP8X4),
@@ -244,15 +262,29 @@ def tile_attend_tab_larger_gains_pl_kernel(
                 start=True,
                 stop=True,
             )
-            cols = slice(r * J, (r + 1) * J)
-            nc.vector.tensor_tensor(y[:, cols], product[:], picked_memory[r][:], MULT)
-            nc.sync.dma_start(y_rows[:, cols], y[:, cols])
-            if r % 2 == 1:
-                nc.vector.tensor_copy(
-                    y_grouped[:].rearrange("p (j t) -> p j t", t=PACK)[:, :, r - 1 : r + 1],
-                    y[:].rearrange("p (t j) -> p j t", t=PACK)[:, :, r - 1 : r + 1],
+            parts = 2 if r == PACK - 1 else 1
+            width = J // parts
+            for h in range(parts):
+                part = slice(h * width, (h + 1) * width)
+                nc.vector.tensor_tensor(
+                    y[:, r * J + part.start : r * J + part.stop], product[:, part], picked_memory[r][:, part], MULT
                 )
-        quantize(y_codes[:], y_scales[:], y_grouped[:])
+            cols = slice(r * J, (r + 1) * J)
+            nc.sync.dma_start(y_rows[:, cols], y[:, cols])
+
+        for u in range(2):
+            planes = (2 * u, 2 * u + 1)
+            turned = [turn(r) for r in planes]
+            if u == 1:
+                group_pair(y_grouped, y, 0)
+            quantized = [quantize_values(r, bank) for r, bank in zip(planes, turned)]
+            for r, (vt_codes, vt_scales) in zip(planes, quantized):
+                multiply(r, vt_codes, vt_scales)
+        halves = [slice(h * J // 2, (h + 1) * J // 2) for h in range(2)]
+        for cols in halves:
+            group_pair(y_grouped, y, 1, cols)
+        for cols in halves:
+            quantize(y_codes[:, cols], y_scales[:, cols], y_grouped[:, PACK * cols.start : PACK * cols.stop])
         nc.sync.dma_start(out_1[0].rearrange("p c r -> p (c r)").bitcast(I32), y_codes[:].bitcast(I32))
         for q in range(4):
             queue = nc.sync if q % 2 == 0 else nc.scalar

@@ -20,10 +20,17 @@ MAX = mybir.AluOpType.max
 
 P = 128
 PACK = 4
+LAST = PACK - 1
+QUADRANTS = 4
+PER_COLUMN = 16
 BANK = 512
+HALF = J // 2
+J_HALVES = (slice(0, HALF), slice(HALF, J))
 ALIGN = 64
 KB = 1024
-PLACES = {
+BANK_BYTES = 2 * KB
+
+SHARED = {
     "ms_grouped1": 0,
     "picked_words": 0,
     "dealt_scales": KB,
@@ -33,9 +40,6 @@ PLACES = {
     "users_picked": 8 * KB,
     "vals_picked0": 8 * KB,
     "vals_picked1": 9 * KB,
-    "vals_raw1": 32 * KB,
-    "vt_grouped0": 32 * KB,
-    "vals_picked2": 32 * KB,
     "gr_grouped": 14 * KB,
     "vt_codes0": 14 * KB,
     "vt_codes1": 14 * KB + KB // 2,
@@ -48,7 +52,12 @@ PLACES = {
     "vals_raw3": 24 * KB,
     "vt_grouped2": 24 * KB,
     "y_grouped": 26 * KB,
+    "vals_raw1": 32 * KB,
+    "vt_grouped0": 32 * KB,
+    "vals_picked2": 32 * KB,
 }
+TURNED_BANK = (0, 1, 1, 0)
+PRODUCT_BANK = (1, 0, 2, 1)
 
 
 def tile_attend_tab_larger_gains_pl_kernel(
@@ -57,184 +66,182 @@ def tile_attend_tab_larger_gains_pl_kernel(
     nc = tc.nc
     with ExitStack() as ctx:
         keep = ctx.enter_context(tc.tile_pool(name="keep", bufs=1))
-        reused = ctx.enter_context(tc.tile_pool(name="reused", bufs=1))
-        psum = ctx.enter_context(tc.psum_pool(name="psum", bufs=1))
-        ring = ctx.enter_context(tc.psum_pool(name="ring", bufs=1))
+        shared = ctx.enter_context(tc.tile_pool(name="shared", bufs=1))
+        wide = ctx.enter_context(tc.psum_pool(name="wide", bufs=4))
+        narrow = ctx.enter_context(tc.psum_pool(name="narrow", bufs=1))
 
         def held(name, shape, dtype):
-            if name in PLACES:
-                return reused.tile(shape, dtype, name=name, align_bytes=ALIGN, offset=PLACES[name])
+            if name in SHARED:
+                return shared.tile(shape, dtype, name=name, align_bytes=ALIGN, offset=SHARED[name])
             return keep.tile(shape, dtype, name=name, align_bytes=ALIGN)
 
-        def gather(engine, out, window, offsets):
-            if engine == "vector":
-                nc.vector.tensor_copy(out, window.indirect(offsets))
+        def gather(on_scalar, target, window, offsets):
+            if on_scalar:
+                nc.scalar.activation(target, window.indirect(offsets), COPY)
             else:
-                nc.scalar.activation(out, window.indirect(offsets), COPY)
+                nc.vector.tensor_copy(target, window.indirect(offsets))
 
         def quantize(codes, scales, grouped):
             nc.vector.quantize_mx(out=codes.bitcast(FP8X4), scales=scales, in_=grouped)
 
-        def group_pair(grouped, planes, u, cols=slice(0, J)):
+        def product(target, lhs, lhs_scales, rhs, rhs_scales):
+            nc.tensor.matmul_mx(
+                out=target, lhsT=lhs, lhsT_scale=lhs_scales, rhs=rhs, rhs_scale=rhs_scales, start=True, stop=True
+            )
+
+        def group_pair(grouped, planes, u, cols):
             nc.vector.tensor_copy(
                 grouped[:].rearrange("p (j t) -> p j t", t=PACK)[:, cols, 2 * u : 2 * u + 2],
                 planes[:].rearrange("p (t j) -> p j t", t=PACK)[:, cols, 2 * u : 2 * u + 2],
             )
 
+        def quantize_halves(codes, scales, grouped):
+            for cols in J_HALVES:
+                quantize(codes[:, cols], scales[:, cols], grouped[:, PACK * cols.start : PACK * cols.stop])
+
         wm_raw = held("wm_raw", [P, PACK * E], F32)
         ms_raw = [held(f"ms_raw{h}", [P, PACK * BANK], F32) for h in range(M // BANK)]
-        list_i = held("list_i", [P, I // 16], U16)
-        list_n = held("list_n", [P, J // 16], U16)
-        list_u = held("list_u", [P, J // 16], U16)
-        list_m = held("list_m", [P, J // 16], U16)
+        list_i = held("list_i", [P, I // PER_COLUMN], U16)
+        list_n = held("list_n", [P, J // PER_COLUMN], U16)
+        list_u = held("list_u", [P, J // PER_COLUMN], U16)
+        list_m = held("list_m", [P, J // PER_COLUMN], U16)
         row_factor = held("row_factor", [P, PACK], F32)
         key_words = held("key_words", [P, T], U16)
         key_scales = held("key_scales", [P, T], U8)
         notes_raw = [held(f"notes_raw{u}", [P, 2 * U], F32) for u in range(2)]
         users_raw = [held(f"users_raw{u}", [P, 2 * Z], F32) for u in range(2)]
-        vals_raw = [held(f"vals_raw{t}", [P, T], F32) for t in range(PACK)]
+        vals_raw = [held(f"vals_raw{r}", [P, T], F32) for r in range(PACK)]
         identity = held("identity", [P, P], F32)
 
         nc.vector.memset(key_scales[:].bitcast(I32), 0)
-        nc.gpsimd.dma_start(row_factor[:], rowf.rearrange("(p t) o -> p (t o)", t=PACK))
+        nc.gpsimd.dma_start(row_factor[:], rowf.rearrange("(p r) o -> p (r o)", r=PACK))
         make_identity(nc, identity[:])
 
-        ms_planes = mstore.rearrange("(p t) (h m) -> h p t m", t=PACK, m=BANK)
+        ms_halves = mstore.rearrange("(p t) (h m) -> h p t m", t=PACK, m=BANK)
         nc.sync.dma_start(wm_raw[:], wm.rearrange("(p t) e -> p (t e)", t=PACK))
-        nc.sync.dma_start(ms_raw[0][:].rearrange("p (t m) -> p t m", t=PACK), ms_planes[0])
+        nc.sync.dma_start(ms_raw[0][:].rearrange("p (t m) -> p t m", t=PACK), ms_halves[0])
         nc.sync.dma_start(list_m[:], offs4)
         nc.sync.dma_start(list_i[:], offs)
         nc.sync.dma_start(list_n[:], offs2)
         nc.sync.dma_start(list_u[:], offs3)
-        nc.sync.dma_start(ms_raw[1][:].rearrange("p (t m) -> p t m", t=PACK), ms_planes[1])
+        nc.sync.dma_start(ms_raw[1][:].rearrange("p (t m) -> p t m", t=PACK), ms_halves[1])
         nc.sync.dma_start(key_words[:].bitcast(I32), keys_words[0].bitcast(I32))
-        for q in range(4):
+        for q in range(QUADRANTS):
             nc.sync.dma_start(
                 key_scales[32 * q : 32 * q + 4, :].bitcast(I32), keys_scales[0, 4 * q : 4 * q + 4, :].bitcast(I32)
             )
         for raw, source in ((notes_raw, notes), (users_raw, users2)):
-            pairs = source.rearrange("(p u e) n -> u p (e n)", u=2, e=2)
+            plane_pairs = source.rearrange("(p u e) n -> u p (e n)", u=2, e=2)
             for u in range(2):
-                nc.sync.dma_start(raw[u][:], pairs[u])
-        vals_planes = vals.rearrange("(p t) n -> t p n", t=PACK)
-        for t in range(PACK):
-            nc.sync.dma_start(vals_raw[t][:], vals_planes[t])
+                nc.sync.dma_start(raw[u][:], plane_pairs[u])
+        vals_planes = vals.rearrange("(p r) n -> r p n", r=PACK)
+        for r in range(PACK):
+            nc.sync.dma_start(vals_raw[r][:], vals_planes[r])
 
         wm_grouped = held("wm_grouped", [P, PACK * E], BF16)
         wm_codes = held("wm_codes", [P, E], U32)
         wm_scales = held("wm_scales", [P, E], U8)
         nc.vector.tensor_copy(
-            wm_grouped[:].rearrange("p (r m t) -> p m r t", r=PACK, t=PACK),
-            wm_raw[:].rearrange("p (t m r) -> p m r t", t=PACK, r=PACK),
+            wm_grouped[:].rearrange("p (r s t) -> p s r t", r=PACK, t=PACK),
+            wm_raw[:].rearrange("p (t s r) -> p s r t", t=PACK, r=PACK),
         )
         quantize(wm_codes[:], wm_scales[:], wm_grouped[:])
 
         memory = [held(f"memory{r}", [P, M], F32) for r in range(PACK)]
         for h in range(M // BANK):
-            cols = slice(h * BANK, (h + 1) * BANK)
             ms_grouped = held(f"ms_grouped{h}", [P, PACK * BANK], BF16)
             ms_codes = held(f"ms_codes{h}", [P, BANK], U32)
             ms_scales = held(f"ms_scales{h}", [P, BANK], U8)
-            target = ms_grouped[:].rearrange("p (m t) -> p m t", t=PACK)
-            source = ms_raw[h][:].rearrange("p (t m) -> p m t", t=PACK)
+            ms_target = ms_grouped[:].rearrange("p (m t) -> p m t", t=PACK)
+            ms_source = ms_raw[h][:].rearrange("p (t m) -> p m t", t=PACK)
             if h == 0:
-                nc.vector.tensor_copy(target[:, : BANK // 2, :], source[:, : BANK // 2, :])
-                nc.scalar.copy(target[:, BANK // 2 :, :], source[:, BANK // 2 :, :])
+                nc.vector.tensor_copy(ms_target[:, : BANK // 2, :], ms_source[:, : BANK // 2, :])
+                nc.scalar.copy(ms_target[:, BANK // 2 :, :], ms_source[:, BANK // 2 :, :])
             else:
-                nc.vector.tensor_copy(target, source)
+                nc.vector.tensor_copy(ms_target, ms_source)
             quantize(ms_codes[:], ms_scales[:], ms_grouped[:])
             for r in range(PACK):
-                rows = slice(r * P, (r + 1) * P)
-                bank = psum.tile([P, BANK], F32, name="bank", tag="wide", bufs=4)
-                nc.tensor.matmul_mx(
-                    out=bank[:],
-                    lhsT=wm_codes[:, rows].bitcast(FP8X4),
-                    lhsT_scale=wm_scales[:, rows],
-                    rhs=ms_codes[:].bitcast(FP8X4),
-                    rhs_scale=ms_scales[:],
-                    start=True,
-                    stop=True,
+                dealt = slice(r * P, (r + 1) * P)
+                bank = wide.tile([P, BANK], F32, name="bank")
+                product(
+                    bank[:], wm_codes[:, dealt].bitcast(FP8X4), wm_scales[:, dealt], ms_codes[:].bitcast(FP8X4), ms_scales[:]
                 )
-                nc.scalar.copy(memory[r][:, cols], bank[:])
+                nc.scalar.copy(memory[r][:, h * BANK : (h + 1) * BANK], bank[:])
 
         picked_words = held("picked_words", [P, I], U16)
         dealt_words = held("dealt_words", [P, I], U16)
         dealt_scales = held("dealt_scales", [P, I], U8)
-        gather("vector", picked_words[:], key_words[:], list_i[:])
-        gather("vector", dealt_scales[:].rearrange("p (r s) -> p s r", r=PACK), key_scales[:], list_i[:])
+        gather(False, picked_words[:], key_words[:], list_i[:])
+        gather(False, dealt_scales[:].rearrange("p (r s) -> p s r", r=PACK), key_scales[:], list_i[:])
         nc.vector.tensor_copy(
             dealt_words[:].rearrange("p (r s) -> p r s", r=PACK), picked_words[:].rearrange("p (s r) -> p r s", r=PACK)
         )
 
-        def scores(name, raw, width, offsets, on_scalar):
+        def scores(name, raw, width, offsets, scalar_planes):
             picked = held(name + "_picked", [P, PACK * J], F32)
             grouped = held(name + "_grouped", [P, PACK * J], BF16)
             codes = held(name + "_codes", [P, J], U32)
             scales = held(name + "_scales", [P, J], U8)
             for t in range(PACK):
-                engine = "scalar" if t in on_scalar else "vector"
-                gather(engine, picked[:, t * J : (t + 1) * J], raw[t // 2][:, t % 2 * width : (t % 2 + 1) * width], offsets)
-                if t % 2 == 1:
-                    group_pair(grouped, picked, t // 2)
-            quantize(codes[:], scales[:], grouped[:])
-            banks = []
-            for pair in range(PACK // 2):
-                bank = psum.tile([P, BANK], F32, name="bank", tag="wide", bufs=4)
-                for half in range(2):
-                    r = 2 * pair + half
-                    slots = slice(r * P, (r + 1) * P)
-                    nc.tensor.matmul_mx(
-                        out=bank[:, half * J : (half + 1) * J],
-                        lhsT=dealt_words[:, slots].bitcast(FP4X4),
-                        lhsT_scale=dealt_scales[:, slots],
-                        rhs=codes[:].bitcast(FP8X4),
-                        rhs_scale=scales[:],
-                        start=True,
-                        stop=True,
+                window = raw[t // 2][:, t % 2 * width : (t % 2 + 1) * width]
+                gather(t in scalar_planes, picked[:, t * J : (t + 1) * J], window, offsets)
+                if t == 1:
+                    group_pair(grouped, picked, 0, slice(0, J))
+            for cols in J_HALVES:
+                group_pair(grouped, picked, 1, cols)
+            quantize_halves(codes, scales, grouped)
+            views = []
+            for cols in J_HALVES:
+                bank = wide.tile([P, BANK], F32, name="bank")
+                for r in range(PACK):
+                    dealt = slice(r * P, (r + 1) * P)
+                    product(
+                        bank[:, r * HALF : (r + 1) * HALF],
+                        dealt_words[:, dealt].bitcast(FP4X4),
+                        dealt_scales[:, dealt],
+                        codes[:, cols].bitcast(FP8X4),
+                        scales[:, cols],
                     )
-                banks.append(bank)
-            return banks
+                views.append(bank[:].rearrange("p (r j) -> p j r", r=PACK))
+            return views
+
+        def by_column(table, cols):
+            return table[:].rearrange("p (j r) -> p j r", r=PACK)[:, cols, :]
 
         g1 = held("g1", [P, PACK * J], F32)
-        for pair, bank in enumerate(scores("notes", notes_raw, U, list_n[:], (1, 3))):
-            nc.scalar.copy(g1[:, pair * BANK : (pair + 1) * BANK], bank[:])
+        for cols, view in zip(J_HALVES, scores("notes", notes_raw, U, list_n[:], (1, LAST))):
+            nc.scalar.copy(by_column(g1, cols), view)
 
         picked_memory = [held(f"picked_memory{r}", [P, J], F32) for r in range(PACK)]
         for r in range(PACK):
-            gather("scalar", picked_memory[r][:], memory[r][:], list_m[:])
+            gather(True, picked_memory[r][:], memory[r][:], list_m[:])
 
         g0 = held("g0", [P, PACK * J], F32)
-        gr_rows = held("gr_rows", [P, PACK * J], BF16)
         gr_grouped = held("gr_grouped", [P, PACK * J], BF16)
         gr_codes = held("gr_codes", [P, J], U32)
         gr_scales = held("gr_scales", [P, J], U8)
-        for pair, bank in enumerate(scores("users", users_raw, Z, list_u[:], (3,))):
-            cols = slice(pair * BANK, (pair + 1) * BANK)
-            nc.vector.tensor_tensor(g0[:, cols], bank[:], g1[:, cols], MAX)
-        for r in range(PACK):
-            cols = slice(r * J, (r + 1) * J)
-            nc.vector.tensor_scalar(gr_rows[:, cols], g0[:, cols], row_factor[:, r : r + 1], None, MULT)
-        nc.vector.tensor_copy(
-            gr_grouped[:].rearrange("p (j t) -> p j t", t=PACK), gr_rows[:].rearrange("p (t j) -> p j t", t=PACK)
-        )
-        quantize(gr_codes[:], gr_scales[:], gr_grouped[:])
+        for cols, view in zip(J_HALVES, scores("users", users_raw, Z, list_u[:], (LAST,))):
+            nc.vector.tensor_tensor(by_column(g0, cols), view, by_column(g1, cols), MAX)
+        factor = row_factor[:].unsqueeze(1).to_broadcast([P, HALF, PACK])
+        for cols in J_HALVES:
+            nc.vector.tensor_tensor(by_column(gr_grouped, cols), by_column(g0, cols), factor, MULT)
+        quantize_halves(gr_codes, gr_scales, gr_grouped)
 
         y = held("y", [P, PACK * J], F32)
         y_grouped = held("y_grouped", [P, PACK * J], BF16)
         y_codes = held("y_codes", [P, J], U32)
         y_scales = held("y_scales", [P, J], U8)
         y_rows = out_0.rearrange("(p r) j -> p (r j)", r=PACK)
-        turned_bank = (0, 1, 1, 0)
-        product_bank = (1, 0, 2, 1)
 
         def turn(r):
             picked = held(f"vals_picked{r}", [P, I], BF16)
-            if r < PACK - 1:
-                gather("scalar", picked[:], vals_raw[r][:], list_i[:])
+            if r == LAST:
+                middle = I // PER_COLUMN // 2
+                gather(False, picked[:, : I // 2], vals_raw[r][:], list_i[:, :middle])
+                gather(True, picked[:, I // 2 :], vals_raw[r][:], list_i[:, middle:])
             else:
-                gather("vector", picked[:, : I // 2], vals_raw[r][:], list_i[:, : I // 32])
-                gather("scalar", picked[:, I // 2 :], vals_raw[r][:], list_i[:, I // 32 :])
-            turned = ring.tile([P, 2 * P], F32, name=f"turned{r}", offset=turned_bank[r] * 2 * KB)
+                gather(True, picked[:], vals_raw[r][:], list_i[:])
+            turned = narrow.tile([P, 2 * P], F32, name=f"turned{r}", offset=TURNED_BANK[r] * BANK_BYTES)
             words = picked[:].bitcast(F32)
             for u in range(2):
                 nc.tensor.transpose(turned[:, u * P : (u + 1) * P], words[:, u::2], identity[:])
@@ -245,48 +252,34 @@ def tile_attend_tab_larger_gains_pl_kernel(
             vt_codes = held(f"vt_codes{r}", [P, P], U32)
             vt_scales = held(f"vt_scales{r}", [P, P], U8)
             nc.scalar.copy(
-                vt_grouped[:].bitcast(F32).rearrange("p (m u) -> p m u", u=2),
-                turned[:].rearrange("p (u m) -> p m u", u=2),
+                vt_grouped[:].bitcast(F32).rearrange("p (s u) -> p s u", u=2),
+                turned[:].rearrange("p (u s) -> p s u", u=2),
             )
             quantize(vt_codes[:], vt_scales[:], vt_grouped[:])
             return vt_codes, vt_scales
 
-        def multiply(r, vt_codes, vt_scales):
-            product = ring.tile([P, J], F32, name=f"product{r}", offset=product_bank[r] * 2 * KB)
-            nc.tensor.matmul_mx(
-                out=product[:],
-                lhsT=vt_codes[:].bitcast(FP8X4),
-                lhsT_scale=vt_scales[:],
-                rhs=gr_codes[:].bitcast(FP8X4),
-                rhs_scale=gr_scales[:],
-                start=True,
-                stop=True,
-            )
-            parts = 2 if r == PACK - 1 else 1
-            width = J // parts
-            for h in range(parts):
-                part = slice(h * width, (h + 1) * width)
-                nc.vector.tensor_tensor(
-                    y[:, r * J + part.start : r * J + part.stop], product[:, part], picked_memory[r][:, part], MULT
-                )
-            cols = slice(r * J, (r + 1) * J)
-            nc.sync.dma_start(y_rows[:, cols], y[:, cols])
+        def result_plane(r, vt_codes, vt_scales):
+            o = narrow.tile([P, J], F32, name=f"o{r}", offset=PRODUCT_BANK[r] * BANK_BYTES)
+            product(o[:], vt_codes[:].bitcast(FP8X4), vt_scales[:], gr_codes[:].bitcast(FP8X4), gr_scales[:])
+            plane = y[:, r * J : (r + 1) * J]
+            for cols in J_HALVES if r == LAST else (slice(0, J),):
+                nc.vector.tensor_tensor(plane[:, cols], o[:, cols], picked_memory[r][:, cols], MULT)
+            nc.sync.dma_start(y_rows[:, r * J : (r + 1) * J], plane)
 
         for u in range(2):
-            planes = (2 * u, 2 * u + 1)
-            turned = [turn(r) for r in planes]
+            pair = (2 * u, 2 * u + 1)
+            turned_pair = [turn(r) for r in pair]
             if u == 1:
-                group_pair(y_grouped, y, 0)
-            quantized = [quantize_values(r, bank) for r, bank in zip(planes, turned)]
-            for r, (vt_codes, vt_scales) in zip(planes, quantized):
-                multiply(r, vt_codes, vt_scales)
-        halves = [slice(h * J // 2, (h + 1) * J // 2) for h in range(2)]
-        for cols in halves:
+                group_pair(y_grouped, y, 0, slice(0, J))
+            quantized = [quantize_values(r, turned) for r, turned in zip(pair, turned_pair)]
+            for r, (vt_codes, vt_scales) in zip(pair, quantized):
+                result_plane(r, vt_codes, vt_scales)
+
+        for cols in J_HALVES:
             group_pair(y_grouped, y, 1, cols)
-        for cols in halves:
-            quantize(y_codes[:, cols], y_scales[:, cols], y_grouped[:, PACK * cols.start : PACK * cols.stop])
+        quantize_halves(y_codes, y_scales, y_grouped)
         nc.sync.dma_start(out_1[0].rearrange("p c r -> p (c r)").bitcast(I32), y_codes[:].bitcast(I32))
-        for q in range(4):
+        for q in range(QUADRANTS):
             queue = nc.sync if q % 2 == 0 else nc.scalar
             queue.dma_start(
                 out_2[0, 4 * q : 4 * q + 4, :].bitcast(I32), y_scales[32 * q : 32 * q + 4, :].bitcast(I32)

@@ -26,6 +26,7 @@ PER_COLUMN = 16
 BANK = 512
 HALF = J // 2
 J_HALVES = (slice(0, HALF), slice(HALF, J))
+WM_SCALAR_SHARE = 40
 ALIGN = 64
 KB = 1024
 BANK_BYTES = 2 * KB
@@ -114,6 +115,10 @@ def tile_attend_tab_larger_gains_pl_kernel(
         identity = held("identity", [P, P], F32)
 
         nc.vector.memset(key_scales[:].bitcast(I32), 0)
+        for q in range(QUADRANTS):
+            nc.gpsimd.dma_start(
+                key_scales[32 * q : 32 * q + 4, :].bitcast(I32), keys_scales[0, 4 * q : 4 * q + 4, :].bitcast(I32)
+            )
         nc.gpsimd.dma_start(row_factor[:], rowf.rearrange("(p r) o -> p (r o)", r=PACK))
         make_identity(nc, identity[:])
 
@@ -126,10 +131,6 @@ def tile_attend_tab_larger_gains_pl_kernel(
         nc.sync.dma_start(list_u[:], offs3)
         nc.sync.dma_start(ms_raw[1][:].rearrange("p (t m) -> p t m", t=PACK), ms_halves[1])
         nc.sync.dma_start(key_words[:].bitcast(I32), keys_words[0].bitcast(I32))
-        for q in range(QUADRANTS):
-            nc.sync.dma_start(
-                key_scales[32 * q : 32 * q + 4, :].bitcast(I32), keys_scales[0, 4 * q : 4 * q + 4, :].bitcast(I32)
-            )
         for raw, source in ((notes_raw, notes), (users_raw, users2)):
             plane_pairs = source.rearrange("(p u e) n -> u p (e n)", u=2, e=2)
             for u in range(2):
@@ -141,10 +142,10 @@ def tile_attend_tab_larger_gains_pl_kernel(
         wm_grouped = held("wm_grouped", [P, PACK * E], BF16)
         wm_codes = held("wm_codes", [P, E], U32)
         wm_scales = held("wm_scales", [P, E], U8)
-        nc.vector.tensor_copy(
-            wm_grouped[:].rearrange("p (r s t) -> p s r t", r=PACK, t=PACK),
-            wm_raw[:].rearrange("p (t s r) -> p s r t", t=PACK, r=PACK),
-        )
+        wm_target = wm_grouped[:].rearrange("p (r s t) -> p s r t", r=PACK, t=PACK)
+        wm_source = wm_raw[:].rearrange("p (t s r) -> p s r t", t=PACK, r=PACK)
+        nc.vector.tensor_copy(wm_target[:, WM_SCALAR_SHARE:], wm_source[:, WM_SCALAR_SHARE:])
+        nc.scalar.copy(wm_target[:, :WM_SCALAR_SHARE], wm_source[:, :WM_SCALAR_SHARE])
         quantize(wm_codes[:], wm_scales[:], wm_grouped[:])
 
         memory = [held(f"memory{r}", [P, M], F32) for r in range(PACK)]

from contextlib import ExitStack

import concourse.mybir as mybir
from concourse.masks import make_identity

D, T, I, J, U, Z, E, M, C = 512, 2048, 512, 256, 1024, 1024, 512, 1024, 512
FLOPS = 2 * (2 * D * I * J + I * E * J + C * E * M)

F32 = mybir.dt.float32
BF16 = mybir.dt.bfloat16
I32 = mybir.dt.int32
U32 = mybir.dt.uint32
U16 = mybir.dt.uint16
U8 = mybir.dt.uint8
FP8X4 = mybir.dt.float8_e4m3fn_x4
FP4X4 = mybir.dt.float4_e2m1fn_x4
COPY = mybir.ActivationFunctionType.Copy
MULT = mybir.AluOpType.mult
MAX = mybir.AluOpType.max

P = 128
PACK = 4
LAST = PACK - 1
QUADRANTS = 4
PER_COLUMN = 16
BANK = 512
HALF = J // 2
J_HALVES = (slice(0, HALF), slice(HALF, J))
WM_SCALAR_SHARE = 40
ALIGN = 64
KB = 1024
BANK_BYTES = 2 * KB

SHARED = {
    "ms_grouped1": 0,
    "picked_words": 0,
    "dealt_scales": KB,
    "ms_codes1": 4 * KB,
    "notes_picked": 4 * KB,
    "notes_grouped": 8 * KB,
    "users_picked": 8 * KB,
    "vals_picked0": 8 * KB,
    "vals_picked1": 9 * KB,
    "gr_grouped": 14 * KB,
    "vt_codes0": 14 * KB,
    "vt_codes1": 14 * KB + KB // 2,
    "notes_raw1": 16 * KB,
    "picked_memory0": 16 * KB,
    "picked_memory2": 17 * KB,
    "picked_memory3": 18 * KB,
    "picked_memory1": 19 * KB,
    "vals_picked3": 19 * KB,
    "vals_raw3": 24 * KB,
    "vt_grouped2": 24 * KB,
    "y_grouped": 26 * KB,
    "vals_raw1": 32 * KB,
    "vt_grouped0": 32 * KB,
    "vals_picked2": 32 * KB,
}
TURNED_BANK = (0, 1, 1, 0)
PRODUCT_BANK = (1, 0, 2, 1)


def tile_attend_tab_larger_gains_pl_kernel(
    tc, keys_words, keys_scales, notes, users2, rowf, vals, wm, mstore, offs, offs2, offs3, offs4, out_0, out_1, out_2
):
    nc = tc.nc
    with ExitStack() as ctx:
        keep = ctx.enter_context(tc.tile_pool(name="keep", bufs=1))
        shared = ctx.enter_context(tc.tile_pool(name="shared", bufs=1))
        wide = ctx.enter_context(tc.psum_pool(name="wide", bufs=4))
        narrow = ctx.enter_context(tc.psum_pool(name="narrow", bufs=1))

        def held(name, shape, dtype):
            if name in SHARED:
                return shared.tile(shape, dtype, name=name, align_bytes=ALIGN, offset=SHARED[name])
            return keep.tile(shape, dtype, name=name, align_bytes=ALIGN)

        def gather(on_scalar, target, window, offsets):
            if on_scalar:
                nc.scalar.activation(target, window.indirect(offsets), COPY)
            else:
                nc.vector.tensor_copy(target, window.indirect(offsets))

        def quantize(codes, scales, grouped):
            nc.vector.quantize_mx(out=codes.bitcast(FP8X4), scales=scales, in_=grouped)

        def product(target, lhs, lhs_scales, rhs, rhs_scales):
            nc.tensor.matmul_mx(
                out=target, lhsT=lhs, lhsT_scale=lhs_scales, rhs=rhs, rhs_scale=rhs_scales, start=True, stop=True
            )

        def group_pair(grouped, planes, u, cols):
            nc.vector.tensor_copy(
                grouped[:].rearrange("p (j t) -> p j t", t=PACK)[:, cols, 2 * u : 2 * u + 2],
                planes[:].rearrange("p (t j) -> p j t", t=PACK)[:, cols, 2 * u : 2 * u + 2],
            )

        def quantize_halves(codes, scales, grouped):
            for cols in J_HALVES:
                quantize(codes[:, cols], scales[:, cols], grouped[:, PACK * cols.start : PACK * cols.stop])

        wm_raw = held("wm_raw", [P, PACK * E], F32)
        ms_raw = [held(f"ms_raw{h}", [P, PACK * BANK], F32) for h in range(M // BANK)]
        list_i = held("list_i", [P, I // PER_COLUMN], U16)
        list_n = held("list_n", [P, J // PER_COLUMN], U16)
        list_u = held("list_u", [P, J // PER_COLUMN], U16)
        list_m = held("list_m", [P, J // PER_COLUMN], U16)
        row_factor = held("row_factor", [P, PACK], F32)
        key_words = held("key_words", [P, T], U16)
        key_scales = held("key_scales", [P, T], U8)
        notes_raw = [held(f"notes_raw{u}", [P, 2 * U], F32) for u in range(2)]
        users_raw = [held(f"users_raw{u}", [P, 2 * Z], F32) for u in range(2)]
        vals_raw = [held(f"vals_raw{r}", [P, T], F32) for r in range(PACK)]
        identity = held("identity", [P, P], F32)

        nc.vector.memset(key_scales[:].bitcast(I32), 0)
        for q in range(QUADRANTS):
            nc.gpsimd.dma_start(
                key_scales[32 * q : 32 * q + 4, :].bitcast(I32), keys_scales[0, 4 * q : 4 * q + 4, :].bitcast(I32)
            )
        nc.gpsimd.dma_start(row_factor[:], rowf.rearrange("(p r) o -> p (r o)", r=PACK))
        make_identity(nc, identity[:])

        ms_halves = mstore.rearrange("(p t) (h m) -> h p t m", t=PACK, m=BANK)
        nc.sync.dma_start(wm_raw[:], wm.rearrange("(p t) e -> p (t e)", t=PACK))
        nc.sync.dma_start(ms_raw[0][:].rearrange("p (t m) -> p t m", t=PACK), ms_halves[0])
        nc.sync.dma_start(list_m[:], offs4)
        nc.sync.dma_start(list_i[:], offs)
        nc.sync.dma_start(list_n[:], offs2)
        nc.sync.dma_start(list_u[:], offs3)
        nc.sync.dma_start(ms_raw[1][:].rearrange("p (t m) -> p t m", t=PACK), ms_halves[1])
        nc.sync.dma_start(key_words[:].bitcast(I32), keys_words[0].bitcast(I32))
        for raw, source in ((notes_raw, notes), (users_raw, users2)):
            plane_pairs = source.rearrange("(p u e) n -> u p (e n)", u=2, e=2)
            for u in range(2):
                nc.sync.dma_start(raw[u][:], plane_pairs[u])
        vals_planes = vals.rearrange("(p r) n -> r p n", r=PACK)
        for r in range(PACK):
            nc.sync.dma_start(vals_raw[r][:], vals_planes[r])

        wm_grouped = held("wm_grouped", [P, PACK * E], BF16)
        wm_codes = held("wm_codes", [P, E], U32)
        wm_scales = held("wm_scales", [P, E], U8)
        wm_target = wm_grouped[:].rearrange("p (r s t) -> p s r t", r=PACK, t=PACK)
        wm_source = wm_raw[:].rearrange("p (t s r) -> p s r t", t=PACK, r=PACK)
        nc.vector.tensor_copy(wm_target[:, WM_SCALAR_SHARE:], wm_source[:, WM_SCALAR_SHARE:])
        nc.scalar.copy(wm_target[:, :WM_SCALAR_SHARE], wm_source[:, :WM_SCALAR_SHARE])
        quantize(wm_codes[:], wm_scales[:], wm_grouped[:])

        memory = [held(f"memory{r}", [P, M], F32) for r in range(PACK)]
        for h in range(M // BANK):
            ms_grouped = held(f"ms_grouped{h}", [P, PACK * BANK], BF16)
            ms_codes = held(f"ms_codes{h}", [P, BANK], U32)
            ms_scales = held(f"ms_scales{h}", [P, BANK], U8)
            ms_target = ms_grouped[:].rearrange("p (m t) -> p m t", t=PACK)
            ms_source = ms_raw[h][:].rearrange("p (t m) -> p m t", t=PACK)
            if h == 0:
                nc.vector.tensor_copy(ms_target[:, : BANK // 2, :], ms_source[:, : BANK // 2, :])
                nc.scalar.copy(ms_target[:, BANK // 2 :, :], ms_source[:, BANK // 2 :, :])
            else:
                nc.vector.tensor_copy(ms_target, ms_source)
            quantize(ms_codes[:], ms_scales[:], ms_grouped[:])
            for r in range(PACK):
                dealt = slice(r * P, (r + 1) * P)
                bank = wide.tile([P, BANK], F32, name="bank")
                product(
                    bank[:], wm_codes[:, dealt].bitcast(FP8X4), wm_scales[:, dealt], ms_codes[:].bitcast(FP8X4), ms_scales[:]
                )
                nc.scalar.copy(memory[r][:, h * BANK : (h + 1) * BANK], bank[:])

        picked_words = held("picked_words", [P, I], U16)
        dealt_words = held("dealt_words", [P, I], U16)
        dealt_scales = held("dealt_scales", [P, I], U8)
        gather(False, picked_words[:], key_words[:], list_i[:])
        gather(False, dealt_scales[:].rearrange("p (r s) -> p s r", r=PACK), key_scales[:], list_i[:])
        nc.vector.tensor_copy(
            dealt_words[:].rearrange("p (r s) -> p r s", r=PACK), picked_words[:].rearrange("p (s r) -> p r s", r=PACK)
        )

        def scores(name, raw, width, offsets, scalar_planes):
            picked = held(name + "_picked", [P, PACK * J], F32)
            grouped = held(name + "_grouped", [P, PACK * J], BF16)
            codes = held(name + "_codes", [P, J], U32)
            scales = held(name + "_scales", [P, J], U8)
            for t in range(PACK):
                window = raw[t // 2][:, t % 2 * width : (t % 2 + 1) * width]
                gather(t in scalar_planes, picked[:, t * J : (t + 1) * J], window, offsets)
                if t == 1:
                    group_pair(grouped, picked, 0, slice(0, J))
            for cols in J_HALVES:
                group_pair(grouped, picked, 1, cols)
            quantize_halves(codes, scales, grouped)
            views = []
            for cols in J_HALVES:
                bank = wide.tile([P, BANK], F32, name="bank")
                for r in range(PACK):
                    dealt = slice(r * P, (r + 1) * P)
                    product(
                        bank[:, r * HALF : (r + 1) * HALF],
                        dealt_words[:, dealt].bitcast(FP4X4),
                        dealt_scales[:, dealt],
                        codes[:, cols].bitcast(FP8X4),
                        scales[:, cols],
                    )
                views.append(bank[:].rearrange("p (r j) -> p j r", r=PACK))
            return views

        def by_column(table, cols):
            return table[:].rearrange("p (j r) -> p j r", r=PACK)[:, cols, :]

        g1 = held("g1", [P, PACK * J], F32)
        for cols, view in zip(J_HALVES, scores("notes", notes_raw, U, list_n[:], (1, LAST))):
            nc.scalar.copy(by_column(g1, cols), view)

        picked_memory = [held(f"picked_memory{r}", [P, J], F32) for r in range(PACK)]
        for r in range(PACK):
            gather(True, picked_memory[r][:], memory[r][:], list_m[:])

        g0 = held("g0", [P, PACK * J], F32)
        gr_grouped = held("gr_grouped", [P, PACK * J], BF16)
        gr_codes = held("gr_codes", [P, J], U32)
        gr_scales = held("gr_scales", [P, J], U8)
        for cols, view in zip(J_HALVES, scores("users", users_raw, Z, list_u[:], (LAST,))):
            nc.vector.tensor_tensor(by_column(g0, cols), view, by_column(g1, cols), MAX)
        factor = row_factor[:].unsqueeze(1).to_broadcast([P, HALF, PACK])
        for cols in J_HALVES:
            nc.vector.tensor_tensor(by_column(gr_grouped, cols), by_column(g0, cols), factor, MULT)
        quantize_halves(gr_codes, gr_scales, gr_grouped)

        y = held("y", [P, PACK * J], F32)
        y_grouped = held("y_grouped", [P, PACK * J], BF16)
        y_codes = held("y_codes", [P, J], U32)
        y_scales = held("y_scales", [P, J], U8)
        y_rows = out_0.rearrange("(p r) j -> p (r j)", r=PACK)

        def turn(r):
            picked = held(f"vals_picked{r}", [P, I], BF16)
            if r == LAST:
                middle = I // PER_COLUMN // 2
                gather(False, picked[:, : I // 2], vals_raw[r][:], list_i[:, :middle])
                gather(True, picked[:, I // 2 :], vals_raw[r][:], list_i[:, middle:])
            else:
                gather(True, picked[:], vals_raw[r][:], list_i[:])
            turned = narrow.tile([P, 2 * P], F32, name=f"turned{r}", offset=TURNED_BANK[r] * BANK_BYTES)
            words = picked[:].bitcast(F32)
            for u in range(2):
                nc.tensor.transpose(turned[:, u * P : (u + 1) * P], words[:, u::2], identity[:])
            return turned

        def quantize_values(r, turned):
            vt_grouped = held(f"vt_grouped{r}", [P, PACK * P], BF16)
            vt_codes = held(f"vt_codes{r}", [P, P], U32)
            vt_scales = held(f"vt_scales{r}", [P, P], U8)
            nc.scalar.copy(
                vt_grouped[:].bitcast(F32).rearrange("p (s u) -> p s u", u=2),
                turned[:].rearrange("p (u s) -> p s u", u=2),
            )
            quantize(vt_codes[:], vt_scales[:], vt_grouped[:])
            return vt_codes, vt_scales

        def result_plane(r, vt_codes, vt_scales):
            o = narrow.tile([P, J], F32, name=f"o{r}", offset=PRODUCT_BANK[r] * BANK_BYTES)
            product(o[:], vt_codes[:].bitcast(FP8X4), vt_scales[:], gr_codes[:].bitcast(FP8X4), gr_scales[:])
            plane = y[:, r * J : (r + 1) * J]
            for cols in J_HALVES if r == LAST else (slice(0, J),):
                nc.vector.tensor_tensor(plane[:, cols], o[:, cols], picked_memory[r][:, cols], MULT)
            nc.sync.dma_start(y_rows[:, r * J : (r + 1) * J], plane)

        for u in range(2):
            pair = (2 * u, 2 * u + 1)
            turned_pair = [turn(r) for r in pair]
            if u == 1:
                group_pair(y_grouped, y, 0, slice(0, J))
            quantized = [quantize_values(r, turned) for r, turned in zip(pair, turned_pair)]
            for r, (vt_codes, vt_scales) in zip(pair, quantized):
                result_plane(r, vt_codes, vt_scales)

        for cols in J_HALVES:
            group_pair(y_grouped, y, 1, cols)
        quantize_halves(y_codes, y_scales, y_grouped)
        nc.sync.dma_start(out_1[0].rearrange("p c r -> p (c r)").bitcast(I32), y_codes[:].bitcast(I32))
        for q in range(QUADRANTS):
            queue = nc.sync if q % 2 == 0 else nc.scalar
            queue.dma_start(
                out_2[0, 4 * q : 4 * q + 4, :].bitcast(I32), y_scales[32 * q : 32 * q + 4, :].bitcast(I32)
            )
